import numpy as np
import ml_dtypes


def mxq(x, axis, fmt="e4m3"):
    dtype, down = {"e4m3": (ml_dtypes.float8_e4m3fn, 7), "e5m2": (ml_dtypes.float8_e5m2, 14)}[fmt]
    v = np.moveaxis(np.asarray(x, np.float32).astype(ml_dtypes.bfloat16).astype(np.float64), axis, -1)
    blocks = v.reshape(v.shape[:-1] + (-1, 32))
    amax = np.abs(blocks).max(-1, keepdims=True)
    byte = np.maximum(np.where(amax > 0, np.frexp(amax)[1] - 1 + 127, 0) - down, 1)
    scale = np.exp2(byte - 127.0)
    codes = (blocks / scale).astype(np.float32).astype(dtype).astype(np.float64)
    return np.moveaxis((codes * scale).reshape(v.shape), -1, axis)


WIDE = False


def mx_kscale(k):
    if not WIDE:
        return np.ones(k)
    levels = np.array([10, -10, 5, -5, 0])
    if k % 512:
        return np.exp2(np.random.permutation(np.resize(levels, k // 32))).repeat(32)
    a = np.empty((k // 512, 16))
    for p in range(k // 512):
        a[p, :8] = np.random.permutation(np.resize(levels, 8))
        for g in range(8):
            far = levels[np.abs(levels - a[p, g]) >= 10]
            a[p, g + 8] = far[np.random.randint(len(far))]
    return np.exp2(a.ravel()).repeat(32)


def f64(x):
    return np.asarray(x).astype(np.float64)


def striped(idx):
    return np.tile(idx.reshape(-1, 16).T, (8, 1)).astype(np.uint16)


def unstriped(offs):
    return offs[:16].T.reshape(-1).astype(np.int64)


E2M1 = np.array([0.0, 0.5, 1.0, 1.5, 2.0, 3.0, 4.0, 6.0, -0.0, -0.5, -1.0, -1.5, -2.0, -3.0, -4.0, -6.0])


def pack_weight(w, fmt):
    k, n = w.shape
    w = f64(np.asarray(w, np.float32).astype(ml_dtypes.bfloat16)).reshape(k // 32, 32, n)
    amax = np.abs(w).max(1)
    if fmt == "e4m3":
        byte = np.frexp(amax)[1] - 1 + 127 - 7
    else:
        mant, ex = np.frexp(amax / 6.0)
        byte = np.where(mant > 0.5, ex, ex - 1) + 127
    byte = np.clip(np.where(amax > 0, byte, 1), 1, 254)
    scaled = (w * np.exp2(127.0 - byte)[:, None, :]).reshape(k, n).astype(np.float32)
    by_word = np.ascontiguousarray(scaled.reshape(k // 512, 128, 4, n).transpose(0, 1, 3, 2))
    if fmt == "e4m3":
        words = by_word.astype(ml_dtypes.float8_e4m3fn).view(np.uint8)
    else:
        c = by_word.astype(ml_dtypes.float4_e2m1fn).view(np.uint8) & 0xF
        words = (c[..., 0::2] | (c[..., 1::2] << 4)).reshape(k // 512, 128, 2 * n)
    return np.ascontiguousarray(words), np.ascontiguousarray(byte.astype(np.uint8).reshape(k // 512, 16, n))


def unpack_weight(words, scales, fmt):
    g, _, n = scales.shape
    words = np.ascontiguousarray(words).reshape(g, 128, n, -1)
    if fmt == "e4m3":
        vals = words.view(ml_dtypes.float8_e4m3fn).astype(np.float64)
    else:
        nib = np.empty((g, 128, n, 4), np.uint8)
        nib[..., 0::2] = words & 0xF
        nib[..., 1::2] = words >> 4
        vals = E2M1[nib]
    vals = vals * np.repeat(np.exp2(scales.astype(np.float64) - 127.0), 8, axis=1)[..., None]
    return vals.transpose(0, 1, 3, 2).reshape(g * 512, n)


def gelu(v):
    return 0.5 * v * (1.0 + np.tanh(np.sqrt(2.0 / np.pi) * (v + 0.044715 * v**3)))


K, T, S, S2 = 1024, 4096, 1024, 512

def setup_inputs():
    n = np.random.standard_normal
    s = mx_kscale(K)[:, None]
    d = {}
    d["tab_words"], d["tab_scales"] = pack_weight(n((K, T)) * s, "e4m3")
    d["offs"] = striped(np.random.permutation(T)[:S])
    d["offs2"] = striped(np.random.permutation(T)[:S2])
    d["w1"] = (1.4 * n((K, K)) / s / s.T / K).astype(np.float32)
    d["b1"] = (0.8 * n(K) / s[:, 0] / K ** 0.5).astype(np.float32)
    d["w4_words"], d["w4_scales"] = pack_weight(n((K, S)) / s / K ** 0.5, "e2m1")
    d["b4"] = (0.7 * n(S2)).astype(np.float32)
    return d

def reference(tab_words, tab_scales, offs, offs2, w1, b1, w4_words, w4_scales, b4):
    TW = unpack_weight(tab_words, tab_scales, "e4m3")
    v = TW[:, unstriped(offs)]
    v2 = TW[:, unstriped(offs2)]
    w4 = unpack_weight(w4_words, w4_scales, "e2m1")
    h = mxq(f64(w1), 0, "e4m3").T @ v
    h = np.maximum(h + f64(b1)[:, None], 0.0)
    e = v2.T @ mxq(h, 0, "e4m3")
    c = v2.T @ w4
    return e + e * (c + f64(b4)[:, None])

@@ -1,0 +1,208 @@
+from contextlib import ExitStack
+
+import concourse.mybir as mybir
+
+K, T, S, S2 = 1024, 4096, 1024, 512
+FLOPS = 2 * K * K * S + 2 * 2 * K * S2 * S
+
+F32 = mybir.dt.float32
+BF16 = mybir.dt.bfloat16
+I32 = mybir.dt.int32
+U32 = mybir.dt.uint32
+U16 = mybir.dt.uint16
+U8 = mybir.dt.uint8
+FP8X4 = mybir.dt.float8_e4m3fn_x4
+FP4X4 = mybir.dt.float4_e2m1fn_x4
+ACT = mybir.ActivationFunctionType
+ALU = mybir.AluOpType
+
+P = 128
+PACK = 4
+KP = P * PACK
+PASSES = K // KP
+N = 512
+HALVES = S // N
+MT = S2 // P
+V_SHARE = {(0, 0): 128, (0, 1): 96, (1, 0): 96, (1, 1): 128}
+
+
+def tile_list_coupler_load_scores_kernel(tc, tab_words, tab_scales, offs, offs2, w1, b1, w4_words, w4_scales, b4, out):
+    nc = tc.nc
+    with ExitStack() as ctx:
+        lists = ctx.enter_context(tc.tile_pool(name="lists", bufs=1))
+        keep = ctx.enter_context(tc.tile_pool(name="keep", bufs=1))
+        early = ctx.enter_context(tc.tile_pool(name="early", bufs=1))
+        psum = ctx.enter_context(tc.psum_pool(name="psum", bufs=4))
+
+        def tile(shape, dtype, name):
+            return keep.tile(shape, dtype, name=name, align_bytes=64)
+
+        o1 = lists.tile([P, S // 16], U16, name="o1")
+        o2 = lists.tile([P, S2 // 16], U16, name="o2")
+        nc.sync.dma_start(o2[:], offs2)
+        nc.sync.dma_start(o1[:], offs)
+
+        tsc = early.tile([P, T], U8, name="tsc", offset=4096, align_bytes=64)
+        nc.vector.memset(tsc[:].bitcast(I32), 0)
+        ts32 = tab_scales.bitcast(I32)
+        for q in range(4):
+            queue = nc.scalar if q % 2 == 0 else nc.gpsimd
+            queue.dma_start(tsc[32 * q : 32 * q + 8, :].bitcast(I32), ts32[:, 4 * q : 4 * q + 4, :])
+
+        tw = []
+        for a in range(PASSES):
+            w = keep.tile([P, T], I32, name="tw%d" % a, tag="big%d" % a, align_bytes=64)
+            nc.sync.dma_start(w[:], tab_words[a].rearrange("p n t -> p (n t)").bitcast(I32))
+            tw.append(w)
+
+        b1t = tile([P, PASSES, PACK], F32, "b1t")
+        nc.scalar.dma_start(b1t[:], b1.rearrange("(b p t) -> p b t", b=PASSES, t=PACK))
+        b4t = tile([P, MT], F32, "b4t")
+        with nc.allow_non_contiguous_dma(reason="one value a partition"):
+            nc.scalar.dma_start(b4t[:], b4.rearrange("(i p) -> p i", p=P))
+        b4p = tile([P, MT], F32, "b4p")
+        nc.scalar.activation(b4p[:], b4t[:], ACT.Identity, bias=1.0)
+
+        w4s = tile([P, PASSES, S], U8, "w4s")
+        nc.vector.memset(w4s[:].bitcast(I32), 0)
+        v2s1 = tile([P, S2], U8, "v2s1")
+        nc.vector.memset(v2s1[:].bitcast(I32), 0)
+        ws32 = w4_scales.bitcast(I32)
+        for q in range(4):
+            nc.gpsimd.dma_start(w4s[32 * q : 32 * q + 4, :, :].bitcast(I32), ws32[:, 4 * q : 4 * q + 4, :].rearrange("a q n -> q a n"))
+
+        v2s = tile([P, S2], U8, "v2s")
+        nc.vector.tensor_copy(v2s[:], tsc[:].indirect(o2[:]))
+        nc.gpsimd.dma_start(v2s1[0 : P - 4, :].bitcast(I32), v2s[4:P, :].bitcast(I32))
+        vs = tile([P, S], U8, "vs")
+        nc.vector.tensor_copy(vs[:], tsc[:].indirect(o1[:]))
+        w4w = early.tile([P, PASSES, 2 * S], U8, name="w4w", offset=6144, align_bytes=64)
+        nc.sync.dma_start(w4w[:].bitcast(I32), w4_words.bitcast(I32).rearrange("a p n -> p a n"))
+        v2w = []
+        vw = {}
+        raw = {}
+        for a in range(PASSES):
+            if a == 0:
+                g = early.tile([P, S2 + S], U32, name="picked0", offset=0, align_bytes=64)
+            else:
+                g = tile([P, S2 + S], U32, "picked1")
+            nc.vector.tensor_copy(g[:, 0:S2], tw[a][:].bitcast(U32).indirect(o2[:]))
+            v2w.append(g[:, 0:S2])
+            for jh in range(HALVES):
+                cols = slice(S2 + N * jh, S2 + N * (jh + 1))
+                nc.vector.tensor_copy(g[:, cols], tw[a][:].bitcast(U32).indirect(o1[:, 32 * jh : 32 * (jh + 1)]))
+                vw[a, jh] = g[:, cols]
+            b = a
+            r = keep.tile([P, PASSES, PACK, KP], F32, name="raw%d" % b, tag="big%d" % b, align_bytes=64)
+            for a2 in range(PASSES):
+                nc.sync.dma_start(r[:, a2], w1[KP * a2 : KP * (a2 + 1), KP * b : KP * (b + 1)].rearrange("(p j) c -> p j c", j=PACK))
+                raw[b, a2] = r[:, a2]
+        v2sc = [v2s, v2s1]
+
+        cp = {}
+
+        def c_unit(i, jh):
+            acc = psum.tile([P, N], F32, name="ep")
+            for a in range(PASSES):
+                nc.tensor.matmul_mx(
+                    out=acc[:],
+                    lhsT=v2w[a][:, P * i : P * (i + 1)].bitcast(FP8X4),
+                    lhsT_scale=v2sc[a][:, P * i : P * (i + 1)],
+                    rhs=w4w[:, a, 2 * N * jh : 2 * N * (jh + 1)].bitcast(FP4X4),
+                    rhs_scale=w4s[:, a, N * jh : N * (jh + 1)],
+                    start=(a == 0),
+                    stop=(a == PASSES - 1),
+                )
+            t = tile([P, N], F32, "cp%d%d" % (i, jh))
+            nc.scalar.activation(t[:], acc[:], ACT.Identity, bias=b4p[:, i : i + 1])
+            cp[i, jh] = t
+
+        wq = {}
+        wqs = {}
+
+        def w1_piece(b, a):
+            g = tile([P, PACK * KP], BF16, "wg%d%d" % (b, a))
+            src = raw[b, a].rearrange("p j (m t) -> p m j t", t=PACK)
+            dst = g[:].rearrange("p (t m j) -> p m j t", t=PACK, j=PACK)
+            mv = V_SHARE[b, a]
+            if mv > 0:
+                nc.vector.tensor_copy(dst[:, 0:mv], src[:, 0:mv])
+            if mv < P:
+                nc.scalar.copy(dst[:, mv:P], src[:, mv:P])
+            codes = tile([P, KP], U32, "wq%d%d" % (b, a))
+            scales = tile([P, KP], U8, "wqs%d%d" % (b, a))
+            nc.vector.quantize_mx(out=codes[:].bitcast(FP8X4), scales=scales[:], in_=g[:])
+            wq[b, a] = codes
+            wqs[b, a] = scales
+
+        hpl = {}
+
+        def h_unit(b, jh):
+            pl = tile([P, PACK, N], BF16, "hpl%d%d" % (b, jh))
+            for t in range(PACK):
+                acc = psum.tile([P, N], F32, name="hp")
+                for a in range(PASSES):
+                    nc.tensor.matmul_mx(
+                        out=acc[:],
+                        lhsT=wq[b, a][:, P * t : P * (t + 1)].bitcast(FP8X4),
+                        lhsT_scale=wqs[b, a][:, P * t : P * (t + 1)],
+                        rhs=vw[a, jh].bitcast(FP8X4),
+                        rhs_scale=vs[4 * a : P, N * jh : N * (jh + 1)],
+                        start=(a == 0),
+                        stop=(a == PASSES - 1),
+                    )
+                nc.scalar.activation(pl[:, t, :], acc[:], ACT.Relu, bias=b1t[:, b, t : t + 1])
+            hpl[b, jh] = pl
+
+        hq = {}
+        hqs = {}
+
+        def h_quant(b, jh, cv):
+            g = tile([P, N * PACK], BF16, "hg%d%d" % (b, jh))
+            src = hpl[b, jh][:].rearrange("p t (c i) -> p c t i", i=4)
+            dst = g[:].rearrange("p (c i t) -> p c t i", i=4, t=PACK)
+            if cv > 0:
+                nc.vector.tensor_copy(dst[:, 0:cv], src[:, 0:cv])
+            if cv < P:
+                nc.scalar.copy(dst[:, cv:P], src[:, cv:P])
+            codes = tile([P, N], U32, "hq%d%d" % (b, jh))
+            scales = tile([P, N], U8, "hqs%d%d" % (b, jh))
+            nc.vector.quantize_mx(out=codes[:].bitcast(FP8X4), scales=scales[:], in_=g[:])
+            hq[b, jh] = codes
+            hqs[b, jh] = scales
+
+        def e_unit(i, jh):
+            acc = psum.tile([P, N], F32, name="ep")
+            for b in range(PASSES):
+                nc.tensor.matmul_mx(
+                    out=acc[:],
+                    lhsT=v2w[b][:, P * i : P * (i + 1)].bitcast(FP8X4),
+                    lhsT_scale=v2sc[b][:, P * i : P * (i + 1)],
+                    rhs=hq[b, jh][:].bitcast(FP8X4),
+                    rhs_scale=hqs[b, jh][:],
+                    start=(b == 0),
+                    stop=(b == PASSES - 1),
+                )
+            res = tile([P, N], F32, "res%d%d" % (i, jh))
+            nc.vector.tensor_tensor(res[:], acc[:], cp[i, jh][:], ALU.mult)
+            nc.sync.dma_start(out[P * i : P * (i + 1), N * jh : N * (jh + 1)], res[:])
+
+        for jh in range(HALVES):
+            for i in range(MT):
+                c_unit(i, jh)
+        w1_piece(0, 0)
+        w1_piece(0, 1)
+        h_unit(0, 0)
+        h_unit(0, 1)
+        w1_piece(1, 0)
+        w1_piece(1, 1)
+        h_unit(1, 0)
+        h_unit(1, 1)
+        h_quant(0, 0, 128)
+        h_quant(0, 1, 128)
+        h_quant(1, 0, 128)
+        for i in range(MT):
+            e_unit(i, 0)
+        h_quant(1, 1, 64)
+        for i in range(MT):
+            e_unit(i, 1)

@@ -23,7 +23,7 @@ PASSES = K // KP
 N = 512
 HALVES = S // N
 MT = S2 // P
-V_SHARE = {(0, 0): 128, (0, 1): 96, (1, 0): 96, (1, 1): 128}
+V_SHARE = {(0, 0): 128, (0, 1): 128, (1, 0): 128, (1, 1): 128}
 
 
 def tile_list_coupler_load_scores_kernel(tc, tab_words, tab_scales, offs, offs2, w1, b1, w4_words, w4_scales, b4, out):
@@ -32,77 +32,91 @@ def tile_list_coupler_load_scores_kernel(tc, tab_words, tab_scales, offs, offs2,
         lists = ctx.enter_context(tc.tile_pool(name="lists", bufs=1))
         keep = ctx.enter_context(tc.tile_pool(name="keep", bufs=1))
         early = ctx.enter_context(tc.tile_pool(name="early", bufs=1))
-        psum = ctx.enter_context(tc.psum_pool(name="psum", bufs=4))
+        stage = ctx.enter_context(tc.tile_pool(name="stage", bufs=2))
+        psum = ctx.enter_context(tc.psum_pool(name="psum", bufs=8))
 
         def tile(shape, dtype, name):
             return keep.tile(shape, dtype, name=name, align_bytes=64)
 
         o1 = lists.tile([P, S // 16], U16, name="o1")
         o2 = lists.tile([P, S2 // 16], U16, name="o2")
+
+        def shared(shape, dtype, name, offset):
+            return early.tile(shape, dtype, name=name, offset=offset, align_bytes=64)
+
+        KB = 1024
+        tsc = shared([P, T], U8, "tsc", 40 * KB)
+        nc.sync.dma_start(tsc[0:32, :].bitcast(I32), tab_scales.bitcast(I32).rearrange("a q n -> (a q) n"))
+        nc.vector.memset(tsc[32:64, :].bitcast(I32), 0)
+        nc.gpsimd.memset(tsc[64:P, :].bitcast(I32), 0)
         nc.sync.dma_start(o2[:], offs2)
         nc.sync.dma_start(o1[:], offs)
+        tw0 = shared([P, T], I32, "tw0", 0)
+        nc.sync.dma_start(tw0[:], tab_words[0].rearrange("p n t -> p (n t)").bitcast(I32))
 
-        tsc = early.tile([P, T], U8, name="tsc", offset=4096, align_bytes=64)
-        nc.vector.memset(tsc[:].bitcast(I32), 0)
-        ts32 = tab_scales.bitcast(I32)
-        for q in range(4):
-            queue = nc.scalar if q % 2 == 0 else nc.gpsimd
-            queue.dma_start(tsc[32 * q : 32 * q + 8, :].bitcast(I32), ts32[:, 4 * q : 4 * q + 4, :])
-
-        tw = []
-        for a in range(PASSES):
-            w = keep.tile([P, T], I32, name="tw%d" % a, tag="big%d" % a, align_bytes=64)
-            nc.sync.dma_start(w[:], tab_words[a].rearrange("p n t -> p (n t)").bitcast(I32))
-            tw.append(w)
-
+        b4t = shared([P, 32], F32, "b4t", 32 * KB - 64)
+        with nc.allow_non_contiguous_dma(reason="one value a partition"):
+            nc.scalar.dma_start(b4t[:, 0:MT], b4.rearrange("(i p) -> p i", p=P))
         b1t = tile([P, PASSES, PACK], F32, "b1t")
         nc.scalar.dma_start(b1t[:], b1.rearrange("(b p t) -> p b t", b=PASSES, t=PACK))
-        b4t = tile([P, MT], F32, "b4t")
-        with nc.allow_non_contiguous_dma(reason="one value a partition"):
-            nc.scalar.dma_start(b4t[:], b4.rearrange("(i p) -> p i", p=P))
-        b4p = tile([P, MT], F32, "b4p")
-        nc.scalar.activation(b4p[:], b4t[:], ACT.Identity, bias=1.0)
 
         w4s = tile([P, PASSES, S], U8, "w4s")
         nc.vector.memset(w4s[:].bitcast(I32), 0)
-        v2s1 = tile([P, S2], U8, "v2s1")
-        nc.vector.memset(v2s1[:].bitcast(I32), 0)
         ws32 = w4_scales.bitcast(I32)
         for q in range(4):
-            nc.gpsimd.dma_start(w4s[32 * q : 32 * q + 4, :, :].bitcast(I32), ws32[:, 4 * q : 4 * q + 4, :].rearrange("a q n -> q a n"))
+            nc.scalar.dma_start(w4s[32 * q : 32 * q + 4, :, :].bitcast(I32), ws32[:, 4 * q : 4 * q + 4, :].rearrange("a q n -> q a n"))
+        planes = []
+        for a in range(PASSES):
+            pl = tile([P, S2 + S], U8, "plane%d" % a)
+            nc.gpsimd.memset(pl[:].bitcast(I32), 0)
+            planes.append(pl)
 
-        v2s = tile([P, S2], U8, "v2s")
-        nc.vector.tensor_copy(v2s[:], tsc[:].indirect(o2[:]))
-        nc.gpsimd.dma_start(v2s1[0 : P - 4, :].bitcast(I32), v2s[4:P, :].bitcast(I32))
-        vs = tile([P, S], U8, "vs")
-        nc.vector.tensor_copy(vs[:], tsc[:].indirect(o1[:]))
-        w4w = early.tile([P, PASSES, 2 * S], U8, name="w4w", offset=6144, align_bytes=64)
-        nc.sync.dma_start(w4w[:].bitcast(I32), w4_words.bitcast(I32).rearrange("a p n -> p a n"))
+        b4p = tile([P, MT], F32, "b4p")
+        nc.scalar.activation(b4p[:], b4t[:, 0:MT], ACT.Identity, bias=1.0)
+
+        tw1 = shared([P, T], I32, "tw1", 16 * KB)
+        nc.sync.dma_start(tw1[:], tab_words[1].rearrange("p n t -> p (n t)").bitcast(I32))
+        tw = [tw0, tw1]
+
+        raw = {}
+
+        def load_w1(b, a, offset):
+            r = shared([P, PACK, KP], F32, "raw%d%d" % (b, a), offset)
+            nc.sync.dma_start(r[:], w1[KP * a : KP * (a + 1), KP * b : KP * (b + 1)].rearrange("(p j) c -> p j c", j=PACK))
+            raw[b, a] = r[:]
+
         v2w = []
         vw = {}
-        raw = {}
-        for a in range(PASSES):
-            if a == 0:
-                g = early.tile([P, S2 + S], U32, name="picked0", offset=0, align_bytes=64)
-            else:
-                g = tile([P, S2 + S], U32, "picked1")
+
+        def gather_words(a, g):
             nc.vector.tensor_copy(g[:, 0:S2], tw[a][:].bitcast(U32).indirect(o2[:]))
             v2w.append(g[:, 0:S2])
             for jh in range(HALVES):
                 cols = slice(S2 + N * jh, S2 + N * (jh + 1))
                 nc.vector.tensor_copy(g[:, cols], tw[a][:].bitcast(U32).indirect(o1[:, 32 * jh : 32 * (jh + 1)]))
                 vw[a, jh] = g[:, cols]
-            b = a
-            r = keep.tile([P, PASSES, PACK, KP], F32, name="raw%d" % b, tag="big%d" % b, align_bytes=64)
-            for a2 in range(PASSES):
-                nc.sync.dma_start(r[:, a2], w1[KP * a2 : KP * (a2 + 1), KP * b : KP * (b + 1)].rearrange("(p j) c -> p j c", j=PACK))
-                raw[b, a2] = r[:, a2]
-        v2sc = [v2s, v2s1]
+
+        rows = tile([P, S2 + S], U8, "rows")
+        nc.vector.tensor_copy(rows[:, 0:S2], tsc[:].indirect(o2[:]))
+        nc.vector.tensor_copy(rows[:, S2 : S2 + S], tsc[:].indirect(o1[:]))
+        w4w = shared([P, PASSES, 2 * S], U8, "w4w", 40 * KB)
+        nc.sync.dma_start(w4w[:].bitcast(I32), w4_words.bitcast(I32).rearrange("a p n -> p a n"))
+        for a in range(PASSES):
+            for r in range(4):
+                nc.scalar.dma_start(planes[a][r:P:32, :].bitcast(I32), rows[16 * a + r : 16 * (a + 1) : 4, :].bitcast(I32))
+
+        gather_words(0, tile([P, S2 + S], U32, "picked0"))
+        load_w1(0, 0, 0)
+        load_w1(0, 1, 8 * KB)
+        gather_words(1, tile([P, S2 + S], U32, "picked1"))
+        load_w1(1, 0, 16 * KB)
+        load_w1(1, 1, 24 * KB)
+        v2sc = planes
 
         cp = {}
 
         def c_unit(i, jh):
-            acc = psum.tile([P, N], F32, name="ep")
+            acc = psum.tile([P, N], F32, name="acc")
             for a in range(PASSES):
                 nc.tensor.matmul_mx(
                     out=acc[:],
@@ -121,9 +135,9 @@ def tile_list_coupler_load_scores_kernel(tc, tab_words, tab_scales, offs, offs2,
         wqs = {}
 
         def w1_piece(b, a):
-            g = tile([P, PACK * KP], BF16, "wg%d%d" % (b, a))
-            src = raw[b, a].rearrange("p j (m t) -> p m j t", t=PACK)
-            dst = g[:].rearrange("p (t m j) -> p m j t", t=PACK, j=PACK)
+            g = stage.tile([P, PACK * KP], BF16, name="woven", align_bytes=64)
+            src = raw[b, a].rearrange("p j (m t) -> p m t j", t=PACK)
+            dst = g[:].rearrange("p (t m j) -> p m t j", t=PACK, j=PACK)
             mv = V_SHARE[b, a]
             if mv > 0:
                 nc.vector.tensor_copy(dst[:, 0:mv], src[:, 0:mv])
@@ -140,14 +154,14 @@ def tile_list_coupler_load_scores_kernel(tc, tab_words, tab_scales, offs, offs2,
         def h_unit(b, jh):
             pl = tile([P, PACK, N], BF16, "hpl%d%d" % (b, jh))
             for t in range(PACK):
-                acc = psum.tile([P, N], F32, name="hp")
+                acc = psum.tile([P, N], F32, name="acc")
                 for a in range(PASSES):
                     nc.tensor.matmul_mx(
                         out=acc[:],
                         lhsT=wq[b, a][:, P * t : P * (t + 1)].bitcast(FP8X4),
                         lhsT_scale=wqs[b, a][:, P * t : P * (t + 1)],
                         rhs=vw[a, jh].bitcast(FP8X4),
-                        rhs_scale=vs[4 * a : P, N * jh : N * (jh + 1)],
+                        rhs_scale=planes[a][:, S2 + N * jh : S2 + N * (jh + 1)],
                         start=(a == 0),
                         stop=(a == PASSES - 1),
                     )
@@ -158,13 +172,14 @@ def tile_list_coupler_load_scores_kernel(tc, tab_words, tab_scales, offs, offs2,
         hqs = {}
 
         def h_quant(b, jh, cv):
-            g = tile([P, N * PACK], BF16, "hg%d%d" % (b, jh))
-            src = hpl[b, jh][:].rearrange("p t (c i) -> p c t i", i=4)
-            dst = g[:].rearrange("p (c i t) -> p c t i", i=4, t=PACK)
+            g = shared([P, N * PACK], BF16, "hg%d%d" % (b, jh), (24 - 8 * b + 4 * jh) * KB)
+            src = hpl[b, jh][:].rearrange("p t c -> p c t")
+            dst = g[:].rearrange("p (c t) -> p c t", t=PACK)
+            cv = 4 * cv
             if cv > 0:
                 nc.vector.tensor_copy(dst[:, 0:cv], src[:, 0:cv])
-            if cv < P:
-                nc.scalar.copy(dst[:, cv:P], src[:, cv:P])
+            if cv < N:
+                nc.scalar.copy(dst[:, cv:N], src[:, cv:N])
             codes = tile([P, N], U32, "hq%d%d" % (b, jh))
             scales = tile([P, N], U8, "hqs%d%d" % (b, jh))
             nc.vector.quantize_mx(out=codes[:].bitcast(FP8X4), scales=scales[:], in_=g[:])
@@ -172,7 +187,7 @@ def tile_list_coupler_load_scores_kernel(tc, tab_words, tab_scales, offs, offs2,
             hqs[b, jh] = scales
 
         def e_unit(i, jh):
-            acc = psum.tile([P, N], F32, name="ep")
+            acc = psum.tile([P, N], F32, name="acc")
             for b in range(PASSES):
                 nc.tensor.matmul_mx(
                     out=acc[:],

@@ -23,7 +23,8 @@ PASSES = K // KP
 N = 512
 HALVES = S // N
 MT = S2 // P
-V_SHARE = {(0, 0): 128, (0, 1): 128, (1, 0): 128, (1, 1): 128}
+V_SHARE = 48
+H_PLACE = {(0, 0, 0): 53, (0, 0, 1): 55, (0, 1, 0): 53, (0, 1, 1): 55, (1, 0, 0): 16, (1, 0, 1): 18, (1, 1, 0): 18}
 
 
 def tile_list_coupler_load_scores_kernel(tc, tab_words, tab_scales, offs, offs2, w1, b1, w4_words, w4_scales, b4, out):
@@ -32,7 +33,6 @@ def tile_list_coupler_load_scores_kernel(tc, tab_words, tab_scales, offs, offs2,
         lists = ctx.enter_context(tc.tile_pool(name="lists", bufs=1))
         keep = ctx.enter_context(tc.tile_pool(name="keep", bufs=1))
         early = ctx.enter_context(tc.tile_pool(name="early", bufs=1))
-        stage = ctx.enter_context(tc.tile_pool(name="stage", bufs=2))
         psum = ctx.enter_context(tc.psum_pool(name="psum", bufs=8))
 
         def tile(shape, dtype, name):
@@ -81,9 +81,14 @@ def tile_list_coupler_load_scores_kernel(tc, tab_words, tab_scales, offs, offs2,
         raw = {}
 
         def load_w1(b, a, offset):
-            r = shared([P, PACK, KP], F32, "raw%d%d" % (b, a), offset)
-            nc.sync.dma_start(r[:], w1[KP * a : KP * (a + 1), KP * b : KP * (b + 1)].rearrange("(p j) c -> p j c", j=PACK))
-            raw[b, a] = r[:]
+            parts = 2 if (b, a) == (1, 1) else 1
+            width = KP // parts
+            raw[b, a] = []
+            for s in range(parts):
+                r = shared([P, PACK, width], F32, "raw%d%d%d" % (b, a, s), offset + s * PACK * width * 4)
+                c0 = KP * b + width * s
+                nc.sync.dma_start(r[:], w1[KP * a : KP * (a + 1), c0 : c0 + width].rearrange("(p j) c -> p j c", j=PACK))
+                raw[b, a].append((r[:], width // PACK * s, width // PACK * (s + 1)))
 
         v2w = []
         vw = {}
@@ -127,7 +132,10 @@ def tile_list_coupler_load_scores_kernel(tc, tab_words, tab_scales, offs, offs2,
                     start=(a == 0),
                     stop=(a == PASSES - 1),
                 )
-            t = tile([P, N], F32, "cp%d%d" % (i, jh))
+            if jh == 1 and i >= 2:
+                t = shared([P, N], F32, "cp%d%d" % (i, jh), (8 + 2 * i) * KB)
+            else:
+                t = tile([P, N], F32, "cp%d%d" % (i, jh))
             nc.scalar.activation(t[:], acc[:], ACT.Identity, bias=b4p[:, i : i + 1])
             cp[i, jh] = t
 
@@ -135,17 +143,22 @@ def tile_list_coupler_load_scores_kernel(tc, tab_words, tab_scales, offs, offs2,
         wqs = {}
 
         def w1_piece(b, a):
-            g = stage.tile([P, PACK * KP], BF16, name="woven", align_bytes=64)
-            src = raw[b, a].rearrange("p j (m t) -> p m t j", t=PACK)
-            dst = g[:].rearrange("p (t m j) -> p m t j", t=PACK, j=PACK)
-            mv = V_SHARE[b, a]
-            if mv > 0:
-                nc.vector.tensor_copy(dst[:, 0:mv], src[:, 0:mv])
-            if mv < P:
-                nc.scalar.copy(dst[:, mv:P], src[:, mv:P])
             codes = tile([P, KP], U32, "wq%d%d" % (b, a))
             scales = tile([P, KP], U8, "wqs%d%d" % (b, a))
-            nc.vector.quantize_mx(out=codes[:].bitcast(FP8X4), scales=scales[:], in_=g[:])
+            halves = []
+            for u in range(2):
+                halves.append(shared([P, 2 * KP], BF16, "wg%d%d%d" % (b, a, u), (46 + 6 * a + 2 * u) * KB))
+            for part, m0, m1 in raw[b, a]:
+                for u in range(2):
+                    src = part.rearrange("p j (m t) -> p m t j", t=PACK)[:, :, 2 * u : 2 * u + 2, :]
+                    dst = halves[u][:].rearrange("p (t m j) -> p m t j", t=2, j=PACK)[:, m0:m1]
+                    mv = V_SHARE if (b, a, u) == (0, 1, 1) else m1 - m0
+                    nc.vector.tensor_copy(dst[:, 0:mv], src[:, 0:mv])
+                    if mv < m1 - m0:
+                        nc.scalar.copy(dst[:, mv:], src[:, mv:])
+            for u in range(2):
+                cols = slice(2 * P * u, 2 * P * (u + 1))
+                nc.vector.quantize_mx(out=codes[:, cols].bitcast(FP8X4), scales=scales[:, cols], in_=halves[u][:])
             wq[b, a] = codes
             wqs[b, a] = scales
 
@@ -171,18 +184,23 @@ def tile_list_coupler_load_scores_kernel(tc, tab_words, tab_scales, offs, offs2,
         hq = {}
         hqs = {}
 
-        def h_quant(b, jh, cv):
-            g = shared([P, N * PACK], BF16, "hg%d%d" % (b, jh), (24 - 8 * b + 4 * jh) * KB)
-            src = hpl[b, jh][:].rearrange("p t c -> p c t")
-            dst = g[:].rearrange("p (c t) -> p c t", t=PACK)
-            cv = 4 * cv
-            if cv > 0:
-                nc.vector.tensor_copy(dst[:, 0:cv], src[:, 0:cv])
-            if cv < N:
-                nc.scalar.copy(dst[:, cv:N], src[:, cv:N])
+        def h_quant(b, jh):
             codes = tile([P, N], U32, "hq%d%d" % (b, jh))
             scales = tile([P, N], U8, "hqs%d%d" % (b, jh))
-            nc.vector.quantize_mx(out=codes[:].bitcast(FP8X4), scales=scales[:], in_=g[:])
+            halves = []
+            for u in range(2):
+                cols = slice(N // 2 * u, N // 2 * (u + 1))
+                src = hpl[b, jh][:, :, cols].rearrange("p t c -> p c t")
+                if (b, jh, u) == (1, 1, 1):
+                    g = shared([P, 2 * N], BF16, "hg111", 20 * KB)
+                    nc.scalar.copy(g[:].rearrange("p (c t) -> p c t", t=PACK), src)
+                else:
+                    g = shared([P, 2 * N], BF16, "hg%d%d%d" % (b, jh, u), H_PLACE[b, jh, u] * KB)
+                    nc.vector.tensor_copy(g[:].rearrange("p (c t) -> p c t", t=PACK), src)
+                halves.append(g)
+            for u in range(2):
+                cols = slice(N // 2 * u, N // 2 * (u + 1))
+                nc.vector.quantize_mx(out=codes[:, cols].bitcast(FP8X4), scales=scales[:, cols], in_=halves[u][:])
             hq[b, jh] = codes
             hqs[b, jh] = scales
 
@@ -198,26 +216,34 @@ def tile_list_coupler_load_scores_kernel(tc, tab_words, tab_scales, offs, offs2,
                     start=(b == 0),
                     stop=(b == PASSES - 1),
                 )
-            res = tile([P, N], F32, "res%d%d" % (i, jh))
+            if (i, jh) == (2, 0):
+                res = shared([P, N], F32, "res20", 20 * KB)
+            else:
+                res = tile([P, N], F32, "res%d%d" % (i, jh))
             nc.vector.tensor_tensor(res[:], acc[:], cp[i, jh][:], ALU.mult)
             nc.sync.dma_start(out[P * i : P * (i + 1), N * jh : N * (jh + 1)], res[:])
 
-        for jh in range(HALVES):
-            for i in range(MT):
-                c_unit(i, jh)
+        for i in range(MT):
+            c_unit(i, 0)
+        c_unit(0, 1)
+        c_unit(1, 1)
         w1_piece(0, 0)
         w1_piece(0, 1)
+        c_unit(2, 1)
+        c_unit(3, 1)
         h_unit(0, 0)
         h_unit(0, 1)
         w1_piece(1, 0)
         w1_piece(1, 1)
         h_unit(1, 0)
         h_unit(1, 1)
-        h_quant(0, 0, 128)
-        h_quant(0, 1, 128)
-        h_quant(1, 0, 128)
-        for i in range(MT):
-            e_unit(i, 0)
-        h_quant(1, 1, 64)
+        h_quant(0, 0)
+        h_quant(0, 1)
+        h_quant(1, 0)
+        e_unit(0, 0)
+        e_unit(1, 0)
+        h_quant(1, 1)
+        e_unit(2, 0)
+        e_unit(3, 0)
         for i in range(MT):
             e_unit(i, 1)

@@ -20,11 +20,25 @@ P = 128
 PACK = 4
 KP = P * PACK
 PASSES = K // KP
+BLOCKS = KP // 32
+QUAD = 32
 N = 512
 HALVES = S // N
 MT = S2 // P
-V_SHARE = 48
-H_PLACE = {(0, 0, 0): 53, (0, 0, 1): 55, (0, 1, 0): 53, (0, 1, 1): 55, (1, 0, 0): 16, (1, 0, 1): 18, (1, 1, 0): 18}
+PER_COLUMN = 16
+LAST = PASSES - 1
+W1_SPLIT = 48
+
+KB = 1024
+AT_W1 = {(1, 0): 0, (0, 0): 8 * KB, (0, 1): 16 * KB, (1, 1): 24 * KB}
+AT_TABLE = [8 * KB - 64, 24 * KB]
+AT_B4 = 40 * KB - 64
+AT_ROWS = 44 * KB
+AT_W4 = [AT_ROWS, 32 * KB]
+AT_W1_WOVEN = [48 * KB, 54 * KB]
+AT_H_WOVEN = [55 * KB, 57 * KB]
+AT_H_ROWS = 60 * KB
+AT_C_LAST = 72 * KB
 
 
 def tile_list_coupler_load_scores_kernel(tc, tab_words, tab_scales, offs, offs2, w1, b1, w4_words, w4_scales, b4, out):
@@ -32,218 +46,204 @@ def tile_list_coupler_load_scores_kernel(tc, tab_words, tab_scales, offs, offs2,
     with ExitStack() as ctx:
         lists = ctx.enter_context(tc.tile_pool(name="lists", bufs=1))
         keep = ctx.enter_context(tc.tile_pool(name="keep", bufs=1))
-        early = ctx.enter_context(tc.tile_pool(name="early", bufs=1))
+        reused = ctx.enter_context(tc.tile_pool(name="reused", bufs=1))
         psum = ctx.enter_context(tc.psum_pool(name="psum", bufs=8))
 
         def tile(shape, dtype, name):
             return keep.tile(shape, dtype, name=name, align_bytes=64)
 
-        o1 = lists.tile([P, S // 16], U16, name="o1")
-        o2 = lists.tile([P, S2 // 16], U16, name="o2")
+        def tile_at(shape, dtype, name, offset):
+            return reused.tile(shape, dtype, name=name, offset=offset, align_bytes=64)
 
-        def shared(shape, dtype, name, offset):
-            return early.tile(shape, dtype, name=name, offset=offset, align_bytes=64)
+        trailing = lists.tile([P, S // PER_COLUMN], U16, name="trailing")
+        leading = lists.tile([P, S2 // PER_COLUMN], U16, name="leading")
 
-        KB = 1024
-        tsc = shared([P, T], U8, "tsc", 40 * KB)
-        nc.sync.dma_start(tsc[0:32, :].bitcast(I32), tab_scales.bitcast(I32).rearrange("a q n -> (a q) n"))
-        nc.vector.memset(tsc[32:64, :].bitcast(I32), 0)
-        nc.gpsimd.memset(tsc[64:P, :].bitcast(I32), 0)
-        nc.sync.dma_start(o2[:], offs2)
-        nc.sync.dma_start(o1[:], offs)
-        tw0 = shared([P, T], I32, "tw0", 0)
-        nc.sync.dma_start(tw0[:], tab_words[0].rearrange("p n t -> p (n t)").bitcast(I32))
+        scale_rows = tile_at([P, T], U8, "scale_rows", AT_ROWS)
+        nc.sync.dma_start(scale_rows[0:QUAD, :].bitcast(I32), tab_scales.bitcast(I32).rearrange("a q n -> (a q) n"))
+        nc.vector.memset(scale_rows[QUAD : 2 * QUAD, :].bitcast(I32), 0)
+        nc.gpsimd.memset(scale_rows[2 * QUAD : P, :].bitcast(I32), 0)
+        nc.sync.dma_start(leading[:], offs2)
+        nc.sync.dma_start(trailing[:], offs)
 
-        b4t = shared([P, 32], F32, "b4t", 32 * KB - 64)
-        with nc.allow_non_contiguous_dma(reason="one value a partition"):
-            nc.scalar.dma_start(b4t[:, 0:MT], b4.rearrange("(i p) -> p i", p=P))
-        b1t = tile([P, PASSES, PACK], F32, "b1t")
-        nc.scalar.dma_start(b1t[:], b1.rearrange("(b p t) -> p b t", b=PASSES, t=PACK))
+        table = []
 
-        w4s = tile([P, PASSES, S], U8, "w4s")
-        nc.vector.memset(w4s[:].bitcast(I32), 0)
-        ws32 = w4_scales.bitcast(I32)
-        for q in range(4):
-            nc.scalar.dma_start(w4s[32 * q : 32 * q + 4, :, :].bitcast(I32), ws32[:, 4 * q : 4 * q + 4, :].rearrange("a q n -> q a n"))
+        def load_table(a):
+            words = tile_at([P, T], I32, "table%d" % a, AT_TABLE[a])
+            nc.sync.dma_start(words[:], tab_words[a].rearrange("p n t -> p (n t)").bitcast(I32))
+            table.append(words)
+
+        load_table(0)
+
+        b4_cols = tile_at([P, MT], F32, "b4_cols", AT_B4)
+        with nc.allow_non_contiguous_dma(reason="one value of b4 for each partition and tile of rows"):
+            nc.scalar.dma_start(b4_cols[:], b4.rearrange("(i p) -> p i", p=P))
+        b1_cols = tile([P, PASSES, PACK], F32, "b1_cols")
+        nc.scalar.dma_start(b1_cols[:], b1.rearrange("(b p t) -> p b t", b=PASSES, t=PACK))
+
+        w4_planes = tile([P, PASSES, S], U8, "w4_planes")
+        nc.vector.memset(w4_planes[:].bitcast(I32), 0)
+        for quad in range(P // QUAD):
+            nc.scalar.dma_start(
+                w4_planes[QUAD * quad : QUAD * quad + 4, :, :].bitcast(I32),
+                w4_scales.bitcast(I32)[:, 4 * quad : 4 * quad + 4, :].rearrange("a q n -> q a n"),
+            )
         planes = []
         for a in range(PASSES):
-            pl = tile([P, S2 + S], U8, "plane%d" % a)
-            nc.gpsimd.memset(pl[:].bitcast(I32), 0)
-            planes.append(pl)
+            plane = tile([P, S2 + S], U8, "plane%d" % a)
+            nc.gpsimd.memset(plane[:].bitcast(I32), 0)
+            planes.append(plane)
 
-        b4p = tile([P, MT], F32, "b4p")
-        nc.scalar.activation(b4p[:], b4t[:, 0:MT], ACT.Identity, bias=1.0)
+        b4_plus_1 = tile([P, MT], F32, "b4_plus_1")
+        nc.scalar.activation(b4_plus_1[:], b4_cols[:], ACT.Identity, bias=1.0)
 
-        tw1 = shared([P, T], I32, "tw1", 16 * KB)
-        nc.sync.dma_start(tw1[:], tab_words[1].rearrange("p n t -> p (n t)").bitcast(I32))
-        tw = [tw0, tw1]
+        load_table(1)
 
-        raw = {}
+        w1_parts = {}
 
-        def load_w1(b, a, offset):
-            parts = 2 if (b, a) == (1, 1) else 1
+        def load_w1(b, a):
+            parts = 2 if (b, a) == (LAST, LAST) else 1
             width = KP // parts
-            raw[b, a] = []
+            w1_parts[b, a] = []
             for s in range(parts):
-                r = shared([P, PACK, width], F32, "raw%d%d%d" % (b, a, s), offset + s * PACK * width * 4)
+                part = tile_at([P, PACK, width], F32, "w1_%d%d%d" % (b, a, s), AT_W1[b, a] + s * PACK * width * 4)
                 c0 = KP * b + width * s
-                nc.sync.dma_start(r[:], w1[KP * a : KP * (a + 1), c0 : c0 + width].rearrange("(p j) c -> p j c", j=PACK))
-                raw[b, a].append((r[:], width // PACK * s, width // PACK * (s + 1)))
+                nc.sync.dma_start(part[:], w1[KP * a : KP * (a + 1), c0 : c0 + width].rearrange("(p j) c -> p j c", j=PACK))
+                w1_parts[b, a].append((part[:], width // PACK * s, width // PACK * (s + 1)))
 
-        v2w = []
-        vw = {}
+        w4_halves = []
 
-        def gather_words(a, g):
-            nc.vector.tensor_copy(g[:, 0:S2], tw[a][:].bitcast(U32).indirect(o2[:]))
-            v2w.append(g[:, 0:S2])
+        def load_w4(jh):
+            words = tile_at([P, PASSES, 2 * N], U8, "w4_%d" % jh, AT_W4[jh])
+            nc.sync.dma_start(words[:].bitcast(I32), w4_words[:, :, 2 * N * jh : 2 * N * (jh + 1)].bitcast(I32).rearrange("a p n -> p a n"))
+            w4_halves.append(words)
+
+        picked = []
+
+        def gather_words(a):
+            words = tile([P, S2 + S], U32, "picked%d" % a)
+            window = table[a][:].bitcast(U32)
+            nc.vector.tensor_copy(words[:, 0:S2], window.indirect(leading[:]))
             for jh in range(HALVES):
-                cols = slice(S2 + N * jh, S2 + N * (jh + 1))
-                nc.vector.tensor_copy(g[:, cols], tw[a][:].bitcast(U32).indirect(o1[:, 32 * jh : 32 * (jh + 1)]))
-                vw[a, jh] = g[:, cols]
+                entries = trailing[:, N // PER_COLUMN * jh : N // PER_COLUMN * (jh + 1)]
+                nc.vector.tensor_copy(words[:, S2 + N * jh : S2 + N * (jh + 1)], window.indirect(entries))
+            picked.append(words)
 
-        rows = tile([P, S2 + S], U8, "rows")
-        nc.vector.tensor_copy(rows[:, 0:S2], tsc[:].indirect(o2[:]))
-        nc.vector.tensor_copy(rows[:, S2 : S2 + S], tsc[:].indirect(o1[:]))
-        w4w = shared([P, PASSES, 2 * S], U8, "w4w", 40 * KB)
-        nc.sync.dma_start(w4w[:].bitcast(I32), w4_words.bitcast(I32).rearrange("a p n -> p a n"))
+        picked_rows = tile([P, S2 + S], U8, "picked_rows")
+        nc.vector.tensor_copy(picked_rows[:, 0:S2], scale_rows[:].indirect(leading[:]))
+        nc.vector.tensor_copy(picked_rows[:, S2 : S2 + S], scale_rows[:].indirect(trailing[:]))
+        load_w4(0)
         for a in range(PASSES):
             for r in range(4):
-                nc.scalar.dma_start(planes[a][r:P:32, :].bitcast(I32), rows[16 * a + r : 16 * (a + 1) : 4, :].bitcast(I32))
+                nc.scalar.dma_start(planes[a][r:P:QUAD, :].bitcast(I32), picked_rows[BLOCKS * a + r : BLOCKS * (a + 1) : 4, :].bitcast(I32))
 
-        gather_words(0, tile([P, S2 + S], U32, "picked0"))
-        load_w1(0, 0, 0)
-        load_w1(0, 1, 8 * KB)
-        gather_words(1, tile([P, S2 + S], U32, "picked1"))
-        load_w1(1, 0, 16 * KB)
-        load_w1(1, 1, 24 * KB)
-        v2sc = planes
+        gather_words(0)
+        load_w1(0, 0)
+        load_w1(0, 1)
+        load_w1(1, 0)
+        gather_words(1)
+        load_w1(1, 1)
+        load_w4(1)
 
-        cp = {}
-
-        def c_unit(i, jh):
+        def product(stationary, moving):
             acc = psum.tile([P, N], F32, name="acc")
             for a in range(PASSES):
                 nc.tensor.matmul_mx(
                     out=acc[:],
-                    lhsT=v2w[a][:, P * i : P * (i + 1)].bitcast(FP8X4),
-                    lhsT_scale=v2sc[a][:, P * i : P * (i + 1)],
-                    rhs=w4w[:, a, 2 * N * jh : 2 * N * (jh + 1)].bitcast(FP4X4),
-                    rhs_scale=w4s[:, a, N * jh : N * (jh + 1)],
+                    lhsT=stationary(a)[0],
+                    lhsT_scale=stationary(a)[1],
+                    rhs=moving(a)[0],
+                    rhs_scale=moving(a)[1],
                     start=(a == 0),
-                    stop=(a == PASSES - 1),
+                    stop=(a == LAST),
                 )
-            if jh == 1 and i >= 2:
-                t = shared([P, N], F32, "cp%d%d" % (i, jh), (8 + 2 * i) * KB)
-            else:
-                t = tile([P, N], F32, "cp%d%d" % (i, jh))
-            nc.scalar.activation(t[:], acc[:], ACT.Identity, bias=b4p[:, i : i + 1])
-            cp[i, jh] = t
+            return acc
 
-        wq = {}
-        wqs = {}
+        def picked_columns(first, count):
+            return lambda a: (picked[a][:, first : first + count].bitcast(FP8X4), planes[a][:, first : first + count])
 
-        def w1_piece(b, a):
-            codes = tile([P, KP], U32, "wq%d%d" % (b, a))
-            scales = tile([P, KP], U8, "wqs%d%d" % (b, a))
-            halves = []
+        factor = {}
+
+        def make_factor(jh, dest):
+            for i in range(MT):
+                acc = product(
+                    picked_columns(P * i, P),
+                    lambda a: (w4_halves[jh][:, a, :].bitcast(FP4X4), w4_planes[:, a, N * jh : N * (jh + 1)]),
+                )
+                nc.scalar.activation(dest[:, i, :], acc[:], ACT.Identity, bias=b4_plus_1[:, i : i + 1])
+            factor[jh] = dest
+
+        def quantise(woven, name):
+            codes = tile([P, N], U32, name + "_codes")
+            scales = tile([P, N], U8, name + "_scales")
             for u in range(2):
-                halves.append(shared([P, 2 * KP], BF16, "wg%d%d%d" % (b, a, u), (46 + 6 * a + 2 * u) * KB))
-            for part, m0, m1 in raw[b, a]:
+                cols = slice(N // 2 * u, N // 2 * (u + 1))
+                nc.vector.quantize_mx(out=codes[:, cols].bitcast(FP8X4), scales=scales[:, cols], in_=woven[u][:])
+            return codes, scales
+
+        w1_mx = {}
+
+        def quantise_w1(b, a):
+            woven = []
+            for u in range(2):
+                woven.append(tile_at([P, 2 * KP], BF16, "w1_woven%d%d%d" % (b, a, u), AT_W1_WOVEN[a] + 2 * KB * u))
+            for part, m0, m1 in w1_parts[b, a]:
                 for u in range(2):
-                    src = part.rearrange("p j (m t) -> p m t j", t=PACK)[:, :, 2 * u : 2 * u + 2, :]
-                    dst = halves[u][:].rearrange("p (t m j) -> p m t j", t=2, j=PACK)[:, m0:m1]
-                    mv = V_SHARE if (b, a, u) == (0, 1, 1) else m1 - m0
-                    nc.vector.tensor_copy(dst[:, 0:mv], src[:, 0:mv])
-                    if mv < m1 - m0:
-                        nc.scalar.copy(dst[:, mv:], src[:, mv:])
-            for u in range(2):
-                cols = slice(2 * P * u, 2 * P * (u + 1))
-                nc.vector.quantize_mx(out=codes[:, cols].bitcast(FP8X4), scales=scales[:, cols], in_=halves[u][:])
-            wq[b, a] = codes
-            wqs[b, a] = scales
+                    src = part.rearrange("p j (m t) -> p m j t", t=PACK)[:, :, :, 2 * u : 2 * u + 2]
+                    dst = woven[u][:].rearrange("p (t m j) -> p m j t", t=2, j=PACK)[:, m0:m1]
+                    if (b, a, u) == (0, 1, 1):
+                        nc.vector.tensor_copy(dst[:, 0:W1_SPLIT], src[:, 0:W1_SPLIT])
+                        nc.scalar.copy(dst[:, W1_SPLIT:], src[:, W1_SPLIT:])
+                    else:
+                        nc.vector.tensor_copy(dst, src)
+            w1_mx[b, a] = quantise(woven, "w1_%d%d" % (b, a))
 
-        hpl = {}
+        h_rows = {}
 
-        def h_unit(b, jh):
-            pl = tile([P, PACK, N], BF16, "hpl%d%d" % (b, jh))
+        def make_h(b, jh):
+            rows = tile_at([P, PACK, N], BF16, "h_rows%d%d" % (b, jh), AT_H_ROWS + 4 * KB * (HALVES * b + jh))
             for t in range(PACK):
-                acc = psum.tile([P, N], F32, name="acc")
-                for a in range(PASSES):
-                    nc.tensor.matmul_mx(
-                        out=acc[:],
-                        lhsT=wq[b, a][:, P * t : P * (t + 1)].bitcast(FP8X4),
-                        lhsT_scale=wqs[b, a][:, P * t : P * (t + 1)],
-                        rhs=vw[a, jh].bitcast(FP8X4),
-                        rhs_scale=planes[a][:, S2 + N * jh : S2 + N * (jh + 1)],
-                        start=(a == 0),
-                        stop=(a == PASSES - 1),
-                    )
-                nc.scalar.activation(pl[:, t, :], acc[:], ACT.Relu, bias=b1t[:, b, t : t + 1])
-            hpl[b, jh] = pl
-
-        hq = {}
-        hqs = {}
-
-        def h_quant(b, jh):
-            codes = tile([P, N], U32, "hq%d%d" % (b, jh))
-            scales = tile([P, N], U8, "hqs%d%d" % (b, jh))
-            halves = []
-            for u in range(2):
-                cols = slice(N // 2 * u, N // 2 * (u + 1))
-                src = hpl[b, jh][:, :, cols].rearrange("p t c -> p c t")
-                if (b, jh, u) == (1, 1, 1):
-                    g = shared([P, 2 * N], BF16, "hg111", 20 * KB)
-                    nc.scalar.copy(g[:].rearrange("p (c t) -> p c t", t=PACK), src)
-                else:
-                    g = shared([P, 2 * N], BF16, "hg%d%d%d" % (b, jh, u), H_PLACE[b, jh, u] * KB)
-                    nc.vector.tensor_copy(g[:].rearrange("p (c t) -> p c t", t=PACK), src)
-                halves.append(g)
-            for u in range(2):
-                cols = slice(N // 2 * u, N // 2 * (u + 1))
-                nc.vector.quantize_mx(out=codes[:, cols].bitcast(FP8X4), scales=scales[:, cols], in_=halves[u][:])
-            hq[b, jh] = codes
-            hqs[b, jh] = scales
-
-        def e_unit(i, jh):
-            acc = psum.tile([P, N], F32, name="acc")
-            for b in range(PASSES):
-                nc.tensor.matmul_mx(
-                    out=acc[:],
-                    lhsT=v2w[b][:, P * i : P * (i + 1)].bitcast(FP8X4),
-                    lhsT_scale=v2sc[b][:, P * i : P * (i + 1)],
-                    rhs=hq[b, jh][:].bitcast(FP8X4),
-                    rhs_scale=hqs[b, jh][:],
-                    start=(b == 0),
-                    stop=(b == PASSES - 1),
+                acc = product(
+                    lambda a: (w1_mx[b, a][0][:, P * t : P * (t + 1)].bitcast(FP8X4), w1_mx[b, a][1][:, P * t : P * (t + 1)]),
+                    picked_columns(S2 + N * jh, N),
                 )
-            if (i, jh) == (2, 0):
-                res = shared([P, N], F32, "res20", 20 * KB)
-            else:
-                res = tile([P, N], F32, "res%d%d" % (i, jh))
-            nc.vector.tensor_tensor(res[:], acc[:], cp[i, jh][:], ALU.mult)
-            nc.sync.dma_start(out[P * i : P * (i + 1), N * jh : N * (jh + 1)], res[:])
+                nc.scalar.activation(rows[:, t, :], acc[:], ACT.Relu, bias=b1_cols[:, b, t : t + 1])
+            h_rows[b, jh] = rows
 
+        h_mx = {}
+
+        def quantise_h(b, jh, places, second_on_scalar):
+            woven = []
+            for u in range(2):
+                src = h_rows[b, jh][:, :, N // 2 * u : N // 2 * (u + 1)].rearrange("p t (c i) -> p c t i", i=4)
+                half = tile_at([P, 2 * N], BF16, "h_woven%d%d%d" % (b, jh, u), places[u])
+                dst = half[:].rearrange("p (c i t) -> p c t i", i=4, t=PACK)
+                if u == 1 and second_on_scalar:
+                    nc.scalar.copy(dst, src)
+                else:
+                    nc.vector.tensor_copy(dst, src)
+                woven.append(half)
+            h_mx[b, jh] = quantise(woven, "h_%d%d" % (b, jh))
+
+        def finish(i, jh, result):
+            acc = product(picked_columns(P * i, P), lambda b: (h_mx[b, jh][0][:].bitcast(FP8X4), h_mx[b, jh][1][:]))
+            nc.vector.tensor_tensor(result[:], acc[:], factor[jh][:, i, :], ALU.mult)
+            nc.sync.dma_start(out[P * i : P * (i + 1), N * jh : N * (jh + 1)], result[:])
+
+        make_factor(0, tile([P, MT, N], F32, "factor0"))
+        for b in range(PASSES):
+            for a in range(PASSES):
+                quantise_w1(b, a)
+            for jh in range(HALVES):
+                make_h(b, jh)
+        make_factor(1, tile_at([P, MT, N], F32, "factor1", AT_C_LAST))
+        for jh in range(HALVES):
+            quantise_h(0, jh, AT_H_WOVEN, False)
+        last_places = [AT_W1[1, 0] + 2 * KB * n for n in range(3)]
+        quantise_h(1, 0, last_places[0:2], False)
+        for i in range(2):
+            finish(i, 0, tile([P, N], F32, "result%d0" % i))
+        quantise_h(1, 1, last_places[1:3], True)
+        finish(2, 0, tile_at([P, N], F32, "result20", last_places[2]))
+        finish(3, 0, tile([P, N], F32, "result30"))
         for i in range(MT):
-            c_unit(i, 0)
-        c_unit(0, 1)
-        c_unit(1, 1)
-        w1_piece(0, 0)
-        w1_piece(0, 1)
-        c_unit(2, 1)
-        c_unit(3, 1)
-        h_unit(0, 0)
-        h_unit(0, 1)
-        w1_piece(1, 0)
-        w1_piece(1, 1)
-        h_unit(1, 0)
-        h_unit(1, 1)
-        h_quant(0, 0)
-        h_quant(0, 1)
-        h_quant(1, 0)
-        e_unit(0, 0)
-        e_unit(1, 0)
-        h_quant(1, 1)
-        e_unit(2, 0)
-        e_unit(3, 0)
-        for i in range(MT):
-            e_unit(i, 1)
+            finish(i, 1, tile([P, N], F32, "result%d1" % i))

from contextlib import ExitStack

import concourse.mybir as mybir

K, T, S, S2 = 1024, 4096, 1024, 512
FLOPS = 2 * K * K * S + 2 * 2 * K * S2 * S

F32 = mybir.dt.float32
BF16 = mybir.dt.bfloat16
I32 = mybir.dt.int32
U32 = mybir.dt.uint32
U16 = mybir.dt.uint16
U8 = mybir.dt.uint8
FP8X4 = mybir.dt.float8_e4m3fn_x4
FP4X4 = mybir.dt.float4_e2m1fn_x4
ACT = mybir.ActivationFunctionType
ALU = mybir.AluOpType

P = 128
PACK = 4
KP = P * PACK
PASSES = K // KP
BLOCKS = KP // 32
QUAD = 32
N = 512
HALVES = S // N
MT = S2 // P
PER_COLUMN = 16
LAST = PASSES - 1
W1_SPLIT = 48

KB = 1024
AT_W1 = {(1, 0): 0, (0, 0): 8 * KB, (0, 1): 16 * KB, (1, 1): 24 * KB}
AT_TABLE = [8 * KB - 64, 24 * KB]
AT_B4 = 40 * KB - 64
AT_ROWS = 44 * KB
AT_W4 = [AT_ROWS, 32 * KB]
AT_W1_WOVEN = [48 * KB, 54 * KB]
AT_H_WOVEN = [55 * KB, 57 * KB]
AT_H_ROWS = 60 * KB
AT_C_LAST = 72 * KB


def tile_list_coupler_load_scores_kernel(tc, tab_words, tab_scales, offs, offs2, w1, b1, w4_words, w4_scales, b4, out):
    nc = tc.nc
    with ExitStack() as ctx:
        lists = ctx.enter_context(tc.tile_pool(name="lists", bufs=1))
        keep = ctx.enter_context(tc.tile_pool(name="keep", bufs=1))
        reused = ctx.enter_context(tc.tile_pool(name="reused", bufs=1))
        psum = ctx.enter_context(tc.psum_pool(name="psum", bufs=8))

        def tile(shape, dtype, name):
            return keep.tile(shape, dtype, name=name, align_bytes=64)

        def tile_at(shape, dtype, name, offset):
            return reused.tile(shape, dtype, name=name, offset=offset, align_bytes=64)

        trailing = lists.tile([P, S // PER_COLUMN], U16, name="trailing")
        leading = lists.tile([P, S2 // PER_COLUMN], U16, name="leading")

        scale_rows = tile_at([P, T], U8, "scale_rows", AT_ROWS)
        nc.sync.dma_start(scale_rows[0:QUAD, :].bitcast(I32), tab_scales.bitcast(I32).rearrange("a q n -> (a q) n"))
        nc.vector.memset(scale_rows[QUAD : 2 * QUAD, :].bitcast(I32), 0)
        nc.gpsimd.memset(scale_rows[2 * QUAD : P, :].bitcast(I32), 0)
        nc.sync.dma_start(leading[:], offs2)
        nc.sync.dma_start(trailing[:], offs)

        table = []

        def load_table(a):
            words = tile_at([P, T], I32, "table%d" % a, AT_TABLE[a])
            nc.sync.dma_start(words[:], tab_words[a].rearrange("p n t -> p (n t)").bitcast(I32))
            table.append(words)

        load_table(0)

        b4_cols = tile_at([P, MT], F32, "b4_cols", AT_B4)
        with nc.allow_non_contiguous_dma(reason="one value of b4 for each partition and tile of rows"):
            nc.scalar.dma_start(b4_cols[:], b4.rearrange("(i p) -> p i", p=P))
        b1_cols = tile([P, PASSES, PACK], F32, "b1_cols")
        nc.scalar.dma_start(b1_cols[:], b1.rearrange("(b p t) -> p b t", b=PASSES, t=PACK))

        w4_planes = tile([P, PASSES, S], U8, "w4_planes")
        nc.vector.memset(w4_planes[:].bitcast(I32), 0)
        for quad in range(P // QUAD):
            nc.scalar.dma_start(
                w4_planes[QUAD * quad : QUAD * quad + 4, :, :].bitcast(I32),
                w4_scales.bitcast(I32)[:, 4 * quad : 4 * quad + 4, :].rearrange("a q n -> q a n"),
            )
        planes = []
        for a in range(PASSES):
            plane = tile([P, S2 + S], U8, "plane%d" % a)
            nc.gpsimd.memset(plane[:].bitcast(I32), 0)
            planes.append(plane)

        b4_plus_1 = tile([P, MT], F32, "b4_plus_1")
        nc.scalar.activation(b4_plus_1[:], b4_cols[:], ACT.Identity, bias=1.0)

        load_table(1)

        w1_parts = {}

        def load_w1(b, a):
            parts = 2 if (b, a) == (LAST, LAST) else 1
            width = KP // parts
            w1_parts[b, a] = []
            for s in range(parts):
                part = tile_at([P, PACK, width], F32, "w1_%d%d%d" % (b, a, s), AT_W1[b, a] + s * PACK * width * 4)
                c0 = KP * b + width * s
                nc.sync.dma_start(part[:], w1[KP * a : KP * (a + 1), c0 : c0 + width].rearrange("(p j) c -> p j c", j=PACK))
                w1_parts[b, a].append((part[:], width // PACK * s, width // PACK * (s + 1)))

        w4_halves = []

        def load_w4(jh):
            words = tile_at([P, PASSES, 2 * N], U8, "w4_%d" % jh, AT_W4[jh])
            nc.sync.dma_start(words[:].bitcast(I32), w4_words[:, :, 2 * N * jh : 2 * N * (jh + 1)].bitcast(I32).rearrange("a p n -> p a n"))
            w4_halves.append(words)

        picked = []

        def gather_words(a):
            words = tile([P, S2 + S], U32, "picked%d" % a)
            window = table[a][:].bitcast(U32)
            nc.vector.tensor_copy(words[:, 0:S2], window.indirect(leading[:]))
            for jh in range(HALVES):
                entries = trailing[:, N // PER_COLUMN * jh : N // PER_COLUMN * (jh + 1)]
                nc.vector.tensor_copy(words[:, S2 + N * jh : S2 + N * (jh + 1)], window.indirect(entries))
            picked.append(words)

        picked_rows = tile([P, S2 + S], U8, "picked_rows")
        nc.vector.tensor_copy(picked_rows[:, 0:S2], scale_rows[:].indirect(leading[:]))
        nc.vector.tensor_copy(picked_rows[:, S2 : S2 + S], scale_rows[:].indirect(trailing[:]))
        load_w4(0)
        for a in range(PASSES):
            for r in range(4):
                nc.scalar.dma_start(planes[a][r:P:QUAD, :].bitcast(I32), picked_rows[BLOCKS * a + r : BLOCKS * (a + 1) : 4, :].bitcast(I32))

        gather_words(0)
        load_w1(0, 0)
        load_w1(0, 1)
        load_w1(1, 0)
        gather_words(1)
        load_w1(1, 1)
        load_w4(1)

        def product(stationary, moving):
            acc = psum.tile([P, N], F32, name="acc")
            for a in range(PASSES):
                nc.tensor.matmul_mx(
                    out=acc[:],
                    lhsT=stationary(a)[0],
                    lhsT_scale=stationary(a)[1],
                    rhs=moving(a)[0],
                    rhs_scale=moving(a)[1],
                    start=(a == 0),
                    stop=(a == LAST),
                )
            return acc

        def picked_columns(first, count):
            return lambda a: (picked[a][:, first : first + count].bitcast(FP8X4), planes[a][:, first : first + count])

        factor = {}

        def make_factor(jh, dest):
            for i in range(MT):
                acc = product(
                    picked_columns(P * i, P),
                    lambda a: (w4_halves[jh][:, a, :].bitcast(FP4X4), w4_planes[:, a, N * jh : N * (jh + 1)]),
                )
                nc.scalar.activation(dest[:, i, :], acc[:], ACT.Identity, bias=b4_plus_1[:, i : i + 1])
            factor[jh] = dest

        def quantise(woven, name):
            codes = tile([P, N], U32, name + "_codes")
            scales = tile([P, N], U8, name + "_scales")
            for u in range(2):
                cols = slice(N // 2 * u, N // 2 * (u + 1))
                nc.vector.quantize_mx(out=codes[:, cols].bitcast(FP8X4), scales=scales[:, cols], in_=woven[u][:])
            return codes, scales

        w1_mx = {}

        def quantise_w1(b, a):
            woven = []
            for u in range(2):
                woven.append(tile_at([P, 2 * KP], BF16, "w1_woven%d%d%d" % (b, a, u), AT_W1_WOVEN[a] + 2 * KB * u))
            for part, m0, m1 in w1_parts[b, a]:
                for u in range(2):
                    src = part.rearrange("p j (m t) -> p m j t", t=PACK)[:, :, :, 2 * u : 2 * u + 2]
                    dst = woven[u][:].rearrange("p (t m j) -> p m j t", t=2, j=PACK)[:, m0:m1]
                    if (b, a, u) == (0, 1, 1):
                        nc.vector.tensor_copy(dst[:, 0:W1_SPLIT], src[:, 0:W1_SPLIT])
                        nc.scalar.copy(dst[:, W1_SPLIT:], src[:, W1_SPLIT:])
                    else:
                        nc.vector.tensor_copy(dst, src)
            w1_mx[b, a] = quantise(woven, "w1_%d%d" % (b, a))

        h_rows = {}

        def make_h(b, jh):
            rows = tile_at([P, PACK, N], BF16, "h_rows%d%d" % (b, jh), AT_H_ROWS + 4 * KB * (HALVES * b + jh))
            for t in range(PACK):
                acc = product(
                    lambda a: (w1_mx[b, a][0][:, P * t : P * (t + 1)].bitcast(FP8X4), w1_mx[b, a][1][:, P * t : P * (t + 1)]),
                    picked_columns(S2 + N * jh, N),
                )
                nc.scalar.activation(rows[:, t, :], acc[:], ACT.Relu, bias=b1_cols[:, b, t : t + 1])
            h_rows[b, jh] = rows

        h_mx = {}

        def quantise_h(b, jh, places, second_on_scalar):
            woven = []
            for u in range(2):
                src = h_rows[b, jh][:, :, N // 2 * u : N // 2 * (u + 1)].rearrange("p t (c i) -> p c t i", i=4)
                half = tile_at([P, 2 * N], BF16, "h_woven%d%d%d" % (b, jh, u), places[u])
                dst = half[:].rearrange("p (c i t) -> p c t i", i=4, t=PACK)
                if u == 1 and second_on_scalar:
                    nc.scalar.copy(dst, src)
                else:
                    nc.vector.tensor_copy(dst, src)
                woven.append(half)
            h_mx[b, jh] = quantise(woven, "h_%d%d" % (b, jh))

        def finish(i, jh, result):
            acc = product(picked_columns(P * i, P), lambda b: (h_mx[b, jh][0][:].bitcast(FP8X4), h_mx[b, jh][1][:]))
            nc.vector.tensor_tensor(result[:], acc[:], factor[jh][:, i, :], ALU.mult)
            nc.sync.dma_start(out[P * i : P * (i + 1), N * jh : N * (jh + 1)], result[:])

        make_factor(0, tile([P, MT, N], F32, "factor0"))
        for b in range(PASSES):
            for a in range(PASSES):
                quantise_w1(b, a)
            for jh in range(HALVES):
                make_h(b, jh)
        make_factor(1, tile_at([P, MT, N], F32, "factor1", AT_C_LAST))
        for jh in range(HALVES):
            quantise_h(0, jh, AT_H_WOVEN, False)
        last_places = [AT_W1[1, 0] + 2 * KB * n for n in range(3)]
        quantise_h(1, 0, last_places[0:2], False)
        for i in range(2):
            finish(i, 0, tile([P, N], F32, "result%d0" % i))
        quantise_h(1, 1, last_places[1:3], True)
        finish(2, 0, tile_at([P, N], F32, "result20", last_places[2]))
        finish(3, 0, tile([P, N], F32, "result30"))
        for i in range(MT):
            finish(i, 1, tile([P, N], F32, "result%d1" % i))
